import numpy as np
import ml_dtypes


def mxq(x, axis, fmt="e4m3"):
    dtype, down = {"e4m3": (ml_dtypes.float8_e4m3fn, 7), "e5m2": (ml_dtypes.float8_e5m2, 14)}[fmt]
    v = np.moveaxis(np.asarray(x, np.float32).astype(ml_dtypes.bfloat16).astype(np.float64), axis, -1)
    blocks = v.reshape(v.shape[:-1] + (-1, 32))
    amax = np.abs(blocks).max(-1, keepdims=True)
    byte = np.maximum(np.where(amax > 0, np.frexp(amax)[1] - 1 + 127, 0) - down, 1)
    scale = np.exp2(byte - 127.0)
    codes = (blocks / scale).astype(np.float32).astype(dtype).astype(np.float64)
    return np.moveaxis((codes * scale).reshape(v.shape), -1, axis)


WIDE = False


def mx_kscale(k):
    if not WIDE:
        return np.ones(k)
    levels = np.array([10, -10, 5, -5, 0])
    if k % 512:
        return np.exp2(np.random.permutation(np.resize(levels, k // 32))).repeat(32)
    a = np.empty((k // 512, 16))
    for p in range(k // 512):
        a[p, :8] = np.random.permutation(np.resize(levels, 8))
        for g in range(8):
            far = levels[np.abs(levels - a[p, g]) >= 10]
            a[p, g + 8] = far[np.random.randint(len(far))]
    return np.exp2(a.ravel()).repeat(32)


def f64(x):
    return np.asarray(x).astype(np.float64)


def striped(idx):
    return np.tile(idx.reshape(-1, 16).T, (8, 1)).astype(np.uint16)


def unstriped(offs):
    return offs[:16].T.reshape(-1).astype(np.int64)


def striped8(idx):
    return np.concatenate([x.reshape(-1, 16).T for x in idx]).astype(np.uint16)


def runs(offs, k):
    lists = np.stack([offs[16 * r : 16 * r + 16].T.reshape(-1) for r in range(8)]).astype(np.int64)
    return lists[np.arange(k) % 512 // 64]


def pack_weight(w):
    k, n = w.shape
    w = f64(np.asarray(w, np.float32).astype(ml_dtypes.bfloat16)).reshape(k // 32, 32, n)
    amax = np.abs(w).max(1)
    byte = np.clip(np.where(amax > 0, np.frexp(amax)[1] - 1 + 127 - 7, 1), 1, 254)
    scaled = (w * np.exp2(127.0 - byte)[:, None, :]).reshape(k, n).astype(np.float32)
    words = np.ascontiguousarray(scaled.reshape(k // 512, 128, 4, n).transpose(0, 1, 3, 2)).astype(ml_dtypes.float8_e4m3fn).view(np.uint8)
    return words, np.ascontiguousarray(byte.astype(np.uint8).reshape(k // 512, 16, n))


def unpack_weight(words, scales):
    g, p, n, _ = words.shape
    vals = np.ascontiguousarray(words).view(ml_dtypes.float8_e4m3fn).astype(np.float64) * np.repeat(np.exp2(scales.astype(np.float64) - 127.0), 8, axis=1)[..., None]
    return vals.transpose(0, 1, 3, 2).reshape(g * 512, n)


E2M1 = np.array([0.0, 0.5, 1.0, 1.5, 2.0, 3.0, 4.0, 6.0, -0.0, -0.5, -1.0, -1.5, -2.0, -3.0, -4.0, -6.0])


def pack_fp4(w):
    k, n = w.shape
    w = f64(np.asarray(w, np.float32).astype(ml_dtypes.bfloat16)).reshape(k // 32, 32, n)
    amax = np.abs(w).max(1)
    mant, ex = np.frexp(amax / 6.0)
    byte = np.clip(np.where(amax > 0, np.where(mant > 0.5, ex, ex - 1) + 127, 1), 1, 254)
    scaled = (w * np.exp2(127.0 - byte)[:, None, :]).reshape(k, n).astype(np.float32)
    c = np.ascontiguousarray(scaled.reshape(k // 512, 128, 4, n).transpose(0, 1, 3, 2)).astype(ml_dtypes.float4_e2m1fn).view(np.uint8) & 0xF
    words = (c[..., 0::2] | (c[..., 1::2] << 4)).reshape(k // 512, 128, 2 * n)
    return np.ascontiguousarray(words), np.ascontiguousarray(byte.astype(np.uint8).reshape(k // 512, 16, n))


def unpack_fp4(words, scales):
    g, _, n = scales.shape
    words = np.ascontiguousarray(words).reshape(g, 128, n, 2)
    nib = np.empty((g, 128, n, 4), np.uint8)
    nib[..., 0::2] = words & 0xF
    nib[..., 1::2] = words >> 4
    vals = E2M1[nib] * np.repeat(np.exp2(scales.astype(np.float64) - 127.0), 8, axis=1)[..., None]
    return vals.transpose(0, 1, 3, 2).reshape(g * 512, n)


def planes(y):
    n, m = y.shape
    v = y.astype(np.float32).astype(ml_dtypes.bfloat16).astype(np.float64).reshape(n // 32, 32, m)
    top = np.abs(v).max(1)
    byte = np.clip(np.where(top > 0, np.frexp(top)[1] - 1 + 127 - 7, 1), 1, 254)
    codes = (v * np.exp2(127.0 - byte)[:, None, :]).reshape(n, m).astype(np.float32).astype(ml_dtypes.float8_e4m3fn).view(np.uint8)
    words = codes.reshape(n // 512, 128, 4, m).transpose(0, 1, 3, 2)
    return np.ascontiguousarray(words), np.ascontiguousarray(byte.astype(np.uint8).reshape(n // 512, 16, m))


K, T, S, N, H = 512, 2048, 512, 512, 512


def setup_inputs():
    n = np.random.standard_normal
    s = mx_kscale(K)[:, None]
    u = mx_kscale(H)
    packed_xT = pack_weight(n((K, T)) * s)
    packed_w1 = pack_fp4(n((K, H)) / np.sqrt(K) / s)
    packed_w2 = pack_fp4(n((H, N)) / np.sqrt(2 * H) / u[:, None])
    packed_w3 = pack_fp4(n((K, N)) / np.sqrt(2 * K) / s)
    return {
        "x_words": packed_xT[0],
        "x_scales": packed_xT[1],
        "w1_words": packed_w1[0],
        "w1_scales": packed_w1[1],
        "tau": np.random.uniform(0.3, 0.9, (H, 1)).astype(np.float32),
        "gn": (np.random.uniform(0.5, 1.5, (H, 1)) * u[:, None]).astype(np.float32),
        "w2_words": packed_w2[0],
        "w2_scales": packed_w2[1],
        "w3_words": packed_w3[0],
        "w3_scales": packed_w3[1],
        "offs": striped(np.random.permutation(T)[:S]),
        "n1": striped8(np.stack([np.random.permutation(S) for _ in range(8)])),
        "n2": striped8(np.stack([np.random.permutation(S) for _ in range(8)])),
        "hz": striped8(np.random.randint(0, T, (8, S))),
        "n3": striped8(np.stack([np.random.permutation(S) for _ in range(8)])),
        "n4": striped8(np.stack([np.random.permutation(S) for _ in range(8)])),
    }


def reference(x_words, x_scales, w1_words, w1_scales, tau, gn, w2_words, w2_scales, w3_words, w3_scales, offs, n1, n2, hz, n3, n4):
    xq = unpack_weight(x_words, x_scales)[:, unstriped(offs)]
    y = unpack_fp4(w1_words, w1_scales).T @ xq
    low = y.min(axis=1, keepdims=True)
    ea = np.exp(f64(tau) * (low - (y[np.arange(H)[:, None], runs(n1, H)])))
    z = f64(gn) * (y - (2.0 * (ea * (y[np.arange(H)[:, None], runs(n2, H)]))))
    x_hz = unpack_weight(x_words, x_scales)[np.arange(K)[:, None], runs(hz, K)]
    h = unpack_fp4(w2_words, w2_scales).T @ mxq(z, 0, "e4m3") + unpack_fp4(w3_words, w3_scales).T @ x_hz
    pa = h[np.arange(N)[:, None], runs(n3, N)]
    kr = np.exp(-0.5 * ((h - pa) ** 2))
    pb = h[np.arange(N)[:, None], runs(n4, N)]
    kr2 = np.exp(-0.5 * ((h - pb) ** 2))
    out_0 = (kr * pa + kr2 * pb) / (kr + kr2 + 0.5)
    return (out_0,) + planes(out_0)

@@ -1,0 +1,254 @@
+from contextlib import ExitStack
+
+import concourse.mybir as mybir
+
+K, T, S, N, H = 512, 2048, 512, 512, 512
+FLOPS = 2 * K * H * S + 2 * H * N * S + 2 * K * N * S
+
+F32 = mybir.dt.float32
+BF16 = mybir.dt.bfloat16
+I32 = mybir.dt.int32
+U32 = mybir.dt.uint32
+U16 = mybir.dt.uint16
+U8 = mybir.dt.uint8
+FP8X4 = mybir.dt.float8_e4m3fn_x4
+FP4X4 = mybir.dt.float4_e2m1fn_x4
+ALU = mybir.AluOpType
+ACT = mybir.ActivationFunctionType
+
+P = 128
+PACK = 4
+QUAD = 32
+GROUP = 16
+Z_CHUNKS = ((0, 256), (256, 384), (384, 512))
+HALVES = ((0, 256), (256, 512))
+
+
+def tile_picked_mixhebzkern_none_po_kernel(
+    tc, x_words, x_scales, w1_words, w1_scales, tau, gn, w2_words, w2_scales, w3_words, w3_scales,
+    offs, n1, n2, hz, n3, n4, out_0, out_1, out_2,
+):
+    nc = tc.nc
+    with ExitStack() as ctx:
+        sb = ctx.enter_context(tc.tile_pool(name="sb", bufs=1))
+        ps = ctx.enter_context(tc.psum_pool(name="ps", bufs=1))
+
+        def sbt(shape, dtype, name):
+            return sb.tile(shape, dtype, name=name, align_bytes=64)
+
+        def load_list(src, name):
+            tile = sbt([P, S // GROUP], U16, name)
+            nc.sync.dma_start(tile[:], src)
+            return tile
+
+        def entries(lst, a, b):
+            return lst[:, a // GROUP : b // GROUP]
+
+        def load_scale_rows(tile, src, places):
+            rows = src[0].bitcast(I32)
+            view = tile[:].bitcast(I32)
+            for r, place in enumerate(places):
+                nc.sync.dma_start(out=view[place:P:QUAD, :], in_=rows[r : 4 * PACK : PACK, :])
+
+        def zeroed(eng, width, name):
+            tile = sbt([P, width], U8, name)
+            eng.memset(tile[:].bitcast(I32), 0)
+            return tile
+
+        def load_words(src, name):
+            tile = sbt([P, 2 * H], U8, name)
+            nc.sync.dma_start(out=tile[:].bitcast(I32), in_=src[0].bitcast(I32))
+            return tile
+
+        def deal_words(raw, name):
+            tile = sbt([P, 2 * H], U8, name)
+            nc.scalar.copy(
+                out=tile[:].bitcast(U16).rearrange("p (t m) -> p t m", t=PACK),
+                in_=raw[:].bitcast(U16).rearrange("p (m t) -> p t m", t=PACK),
+            )
+            return tile
+
+        def deal_scales(eng, raw, name):
+            tile = sbt([P, H], U8, name)
+            eng.tensor_copy(
+                out=tile[:].rearrange("p (t m) -> p t m", t=PACK),
+                in_=raw[:].rearrange("p (m t) -> p t m", t=PACK),
+            )
+            return tile
+
+        def interleave(copy, dst, src):
+            copy(
+                out=dst.rearrange("p (c i) t -> p c t i", i=4),
+                in_=src.rearrange("p t (c i) -> p c t i", i=4),
+            )
+
+        xs_plain = zeroed(nc.vector, T, "xs_plain")
+        w1s_raw = zeroed(nc.vector, H, "w1s_raw")
+        xs_runs = zeroed(nc.gpsimd, T, "xs_runs")
+        w3s_raw = zeroed(nc.gpsimd, H, "w3s_raw")
+        w2s_raw = zeroed(nc.gpsimd, H, "w2s_raw")
+        hz_scales = zeroed(nc.gpsimd, S, "hz_scales")
+
+        xw = sbt([P, T], U32, "xw")
+        nc.sync.dma_start(out=xw[:].bitcast(I32), in_=x_words[0].rearrange("p n t -> p (n t)").bitcast(I32))
+        load_scale_rows(xs_plain, x_scales, (0, 1, 2, 3))
+        offs_t = load_list(offs, "offs_t")
+        load_scale_rows(w1s_raw, w1_scales, (0, 1, 2, 3))
+        w1w_raw = load_words(w1_words, "w1w_raw")
+        tau_t = sbt([P, PACK], F32, "tau_t")
+        nc.sync.dma_start(out=tau_t[:], in_=tau.rearrange("(p t) o -> p (t o)", t=PACK))
+        n2_t = load_list(n2, "n2_t")
+        n1_t = load_list(n1, "n1_t")
+        hz_t = load_list(hz, "hz_t")
+        load_scale_rows(xs_runs, x_scales, (0, 1, GROUP, GROUP + 1))
+        gn_t = sbt([P, PACK], F32, "gn_t")
+        nc.sync.dma_start(out=gn_t[:], in_=gn.rearrange("(p t) o -> p (t o)", t=PACK))
+        load_scale_rows(w3s_raw, w3_scales, (0, 1, 2, 3))
+        load_scale_rows(w2s_raw, w2_scales, (0, 1, 2, 3))
+        w3w_raw = load_words(w3_words, "w3w_raw")
+        w2w_raw = load_words(w2_words, "w2w_raw")
+        n3_t = load_list(n3, "n3_t")
+        n4_t = load_list(n4, "n4_t")
+
+        xq_s = sbt([P, S], U8, "xq_s")
+        nc.vector.tensor_copy(xq_s[:], xs_plain[:].indirect(offs_t[:]))
+        w1s = deal_scales(nc.vector, w1s_raw, "w1s")
+        w1w = deal_words(w1w_raw, "w1w")
+        xq_w = sbt([P, S], U32, "xq_w")
+        nc.vector.tensor_copy(xq_w[:], xw[:].indirect(offs_t[:]))
+        neg_tau = sbt([P, PACK], F32, "neg_tau")
+        nc.scalar.activation(out=neg_tau[:], in_=tau_t[:], func=ACT.Copy, scale=-1.0)
+
+        def mx(out, ww, ws, t, rw, rs, start, stop):
+            nc.tensor.matmul_mx(
+                out=out,
+                lhsT=ww[:, 2 * P * t : 2 * P * (t + 1)].bitcast(FP4X4),
+                lhsT_scale=ws[:, P * t : P * (t + 1)],
+                rhs=rw.bitcast(FP8X4),
+                rhs_scale=rs,
+                start=start,
+                stop=stop,
+            )
+
+        y, ea_bias = [], []
+        for t in range(PACK):
+            bank = ps.tile([P, S], F32, name=f"y_bank{t}")
+            mx(bank[:], w1w, w1s, t, xq_w[:], xq_s[:], True, True)
+            yt = sbt([P, S], F32, f"y{t}")
+            low = sbt([P, 1], F32, f"low{t}")
+            nc.vector.tensor_scalar(out=yt[:], in0=bank[:], scalar1=1.0, scalar2=None, op0=ALU.mult, op1=ALU.min, accum_out=low[:])
+            bias = sbt([P, 1], F32, f"ea_bias{t}")
+            nc.vector.tensor_tensor(out=bias[:], in0=low[:], in1=tau_t[:, t : t + 1], op=ALU.mult)
+            y.append(yt)
+            ea_bias.append(bias)
+
+        gn_m2 = sbt([P, PACK], F32, "gn_m2")
+        nc.vector.tensor_scalar(out=gn_m2[:], in0=gn_t[:], scalar1=-2.0, scalar2=None, op0=ALU.mult)
+
+        hz_bytes = sbt([P, S], U8, "hz_bytes")
+        nc.vector.tensor_copy(hz_bytes[:], xs_runs[:].indirect(hz_t[:]))
+        for r, place in enumerate((0, 1, GROUP, GROUP + 1)):
+            nc.sync.dma_start(out=hz_scales[:].bitcast(I32)[r:P:QUAD, :], in_=hz_bytes[:].bitcast(I32)[place:P:QUAD, :])
+        hz_w = sbt([P, S], U32, "hz_w")
+        nc.vector.tensor_copy(hz_w[:], xw[:].indirect(hz_t[:]))
+        w3s = deal_scales(nc.gpsimd, w3s_raw, "w3s")
+        w2s = deal_scales(nc.gpsimd, w2s_raw, "w2s")
+        w3w = deal_words(w3w_raw, "w3w")
+        w2w = deal_words(w2w_raw, "w2w")
+
+        h = [sbt([P, S], F32, f"h{t}") for t in range(PACK)]
+        for c, (a, b) in enumerate(Z_CHUNKS):
+            w = b - a
+            zb = sbt([P, PACK, w], BF16, f"zb{c}")
+            for t in range(PACK):
+                y2 = sbt([P, w], F32, f"y2_{c}_{t}")
+                nc.scalar.activation(out=y2[:], in_=y[t][:].indirect(entries(n2_t, a, b)), func=ACT.Copy)
+                ea = sbt([P, w], F32, f"ea_{c}_{t}")
+                nc.scalar.activation(
+                    out=ea[:], in_=y[t][:].indirect(entries(n1_t, a, b)), func=ACT.Exp,
+                    bias=ea_bias[t][:], scale=neg_tau[:, t : t + 1],
+                )
+                m = sbt([P, w], F32, f"m_{c}_{t}")
+                nc.vector.scalar_tensor_tensor(out=m[:], in0=ea[:], scalar=gn_m2[:, t : t + 1], in1=y2[:], op0=ALU.mult, op1=ALU.mult)
+                nc.vector.scalar_tensor_tensor(out=zb[:, t, :], in0=y[t][:, a:b], scalar=gn_t[:, t : t + 1], in1=m[:], op0=ALU.mult, op1=ALU.add)
+            zi = sbt([P, w, PACK], BF16, f"zi{c}")
+            interleave(nc.vector.tensor_copy, zi[:], zb[:])
+            zq = sbt([P, w], U32, f"zq{c}")
+            zs = sbt([P, w], U8, f"zs{c}")
+            nc.vector.quantize_mx(out=zq[:].bitcast(FP8X4), scales=zs[:], in_=zi[:].rearrange("p n t -> p (n t)"))
+            per_bank = S // w
+            for t0 in range(0, PACK, per_bank):
+                bank = ps.tile([P, per_bank, w], F32, name=f"h_bank{c}_{t0}")
+                for t in range(t0, t0 + per_bank):
+                    mx(bank[:, t - t0, :], w3w, w3s, t, hz_w[:, a:b], hz_scales[:, a:b], True, False)
+                    mx(bank[:, t - t0, :], w2w, w2s, t, zq[:], zs[:], False, True)
+                for t in range(t0, t0 + per_bank):
+                    nc.scalar.copy(out=h[t][:, a:b], in_=bank[:, t - t0, :])
+
+        num = sbt([P, PACK, S], F32, "num")
+        den2 = sbt([P, PACK, S], F32, "den2")
+        pp, kr = [], []
+
+        def fetch(t):
+            pair = sbt([P, 2, S], F32, f"pp{t}")
+            for a, b in HALVES:
+                nc.vector.tensor_copy(pair[:, 0, a:b], h[t][:].indirect(entries(n3_t, a, b)))
+                nc.scalar.activation(out=pair[:, 1, a:b], in_=h[t][:].indirect(entries(n4_t, a, b)), func=ACT.Copy)
+            d = sbt([P, 2, S], F32, f"d{t}")
+            for e in range(2):
+                nc.vector.tensor_tensor(out=d[:, e, :], in0=pair[:, e, :], in1=h[t][:], op=ALU.subtract)
+            pp.append((pair, d))
+
+        def weights(t):
+            d = pp[t][1]
+            sq = sbt([P, 2, S], F32, f"sq{t}")
+            nc.scalar.activation(out=sq[:], in_=d[:], func=ACT.Square)
+            k = sbt([P, 2, S], F32, f"kr{t}")
+            nc.scalar.activation(out=k[:], in_=sq[:], func=ACT.Exp, scale=-0.5)
+            kr.append(k)
+
+        def combine(t):
+            k = kr[t]
+            s = sbt([P, S], F32, f"s{t}")
+            nc.vector.scalar_tensor_tensor(out=s[:], in0=k[:, 0, :], scalar=0.5, in1=k[:, 1, :], op0=ALU.add, op1=ALU.add)
+            if t < PACK - 1:
+                nc.scalar.activation(out=den2[:, t, :], in_=s[:], func=ACT.Square)
+            else:
+                nc.vector.tensor_tensor(out=den2[:, t, :], in0=s[:], in1=s[:], op=ALU.mult)
+            prod = sbt([P, 2, S], F32, f"prod{t}")
+            nc.vector.tensor_tensor(out=prod[:], in0=k[:], in1=pp[t][0][:], op=ALU.mult)
+            nc.vector.tensor_tensor(out=num[:, t, :], in0=prod[:, 0, :], in1=prod[:, 1, :], op=ALU.add)
+
+        fetch(0)
+        fetch(1)
+        weights(0)
+        fetch(2)
+        weights(1)
+        combine(0)
+        fetch(3)
+        weights(2)
+        combine(1)
+        weights(3)
+        combine(2)
+        combine(3)
+
+        out0_v = out_0.rearrange("(p t) j -> p t j", t=PACK)
+        words_v = out_1[0].rearrange("p n t -> p (n t)").bitcast(I32)
+        oq = sbt([P, S], U32, "oq")
+        os_ = sbt([P, S], U8, "os_")
+        for c, (a, b) in enumerate(HALVES):
+            w = b - a
+            rec = sbt([P, PACK, w], F32, f"rec{c}")
+            nc.scalar.activation(out=rec[:], in_=den2[:, :, a:b], func=ACT.Abs_reciprocal_sqrt)
+            o = sbt([P, PACK, w], F32, f"o{c}")
+            nc.vector.tensor_tensor(out=o[:], in0=num[:, :, a:b], in1=rec[:], op=ALU.mult)
+            nc.sync.dma_start(out=out0_v[:, :, a:b], in_=o[:])
+            oi = sbt([P, w, PACK], BF16, f"oi{c}")
+            interleave(nc.scalar.copy if c == 0 else nc.vector.tensor_copy, oi[:], o[:])
+            nc.vector.quantize_mx(out=oq[:, a:b].bitcast(FP8X4), scales=os_[:, a:b], in_=oi[:].rearrange("p n t -> p (n t)"))
+            nc.sync.dma_start(out=words_v[:, a:b], in_=oq[:, a:b].bitcast(I32))
+        for q in range(P // QUAD):
+            nc.sync.dma_start(
+                out=out_2[0].bitcast(I32)[PACK * q : PACK * (q + 1), :],
+                in_=os_[:].bitcast(I32)[QUAD * q : QUAD * q + PACK, :],
+            )

@@ -22,6 +22,7 @@ QUAD = 32
 GROUP = 16
 Z_CHUNKS = ((0, 256), (256, 384), (384, 512))
 HALVES = ((0, 256), (256, 512))
+OUT_CHUNKS = 4
 
 
 def tile_picked_mixhebzkern_none_po_kernel(
@@ -44,20 +45,20 @@ def tile_picked_mixhebzkern_none_po_kernel(
         def entries(lst, a, b):
             return lst[:, a // GROUP : b // GROUP]
 
-        def load_scale_rows(tile, src, places):
+        def load_scale_rows(tile, src, places, queues=(nc.sync,) * PACK):
             rows = src[0].bitcast(I32)
             view = tile[:].bitcast(I32)
             for r, place in enumerate(places):
-                nc.sync.dma_start(out=view[place:P:QUAD, :], in_=rows[r : 4 * PACK : PACK, :])
+                queues[r].dma_start(out=view[place:P:QUAD, :], in_=rows[r : 4 * PACK : PACK, :])
 
         def zeroed(eng, width, name):
             tile = sbt([P, width], U8, name)
             eng.memset(tile[:].bitcast(I32), 0)
             return tile
 
-        def load_words(src, name):
+        def load_words(src, name, queue=nc.sync):
             tile = sbt([P, 2 * H], U8, name)
-            nc.sync.dma_start(out=tile[:].bitcast(I32), in_=src[0].bitcast(I32))
+            queue.dma_start(out=tile[:].bitcast(I32), in_=src[0].bitcast(I32))
             return tile
 
         def deal_words(raw, name):
@@ -82,38 +83,37 @@ def tile_picked_mixhebzkern_none_po_kernel(
                 in_=src.rearrange("p t (c i) -> p c t i", i=4),
             )
 
-        xs_plain = zeroed(nc.vector, T, "xs_plain")
+        xs_plain = zeroed(nc.gpsimd, T, "xs_plain")
         w1s_raw = zeroed(nc.vector, H, "w1s_raw")
-        xs_runs = zeroed(nc.gpsimd, T, "xs_runs")
-        w3s_raw = zeroed(nc.gpsimd, H, "w3s_raw")
-        w2s_raw = zeroed(nc.gpsimd, H, "w2s_raw")
-        hz_scales = zeroed(nc.gpsimd, S, "hz_scales")
+        xs_runs = zeroed(nc.vector, T, "xs_runs")
+        w3s_raw = zeroed(nc.vector, H, "w3s_raw")
+        w2s_raw = zeroed(nc.vector, H, "w2s_raw")
+        hz_scales = zeroed(nc.vector, S, "hz_scales")
 
+        on_scalar = (nc.scalar,) * PACK
+        offs_t = load_list(offs, "offs_t")
+        w1w_raw = load_words(w1_words, "w1w_raw")
         xw = sbt([P, T], U32, "xw")
         nc.sync.dma_start(out=xw[:].bitcast(I32), in_=x_words[0].rearrange("p n t -> p (n t)").bitcast(I32))
-        load_scale_rows(xs_plain, x_scales, (0, 1, 2, 3))
-        offs_t = load_list(offs, "offs_t")
-        load_scale_rows(w1s_raw, w1_scales, (0, 1, 2, 3))
-        w1w_raw = load_words(w1_words, "w1w_raw")
+        load_scale_rows(xs_plain, x_scales, (0, 1, 2, 3), on_scalar)
+        w1w = deal_words(w1w_raw, "w1w")
+        load_scale_rows(w1s_raw, w1_scales, (0, 1, 2, 3), (nc.scalar, nc.sync, nc.sync, nc.sync))
+        hz_t = load_list(hz, "hz_t")
+        w3w = deal_words(load_words(w3_words, "w3w_raw", nc.scalar), "w3w")
+        w2w = deal_words(load_words(w2_words, "w2w_raw", nc.scalar), "w2w")
+        n2_t = load_list(n2, "n2_t")
         tau_t = sbt([P, PACK], F32, "tau_t")
         nc.sync.dma_start(out=tau_t[:], in_=tau.rearrange("(p t) o -> p (t o)", t=PACK))
-        n2_t = load_list(n2, "n2_t")
         n1_t = load_list(n1, "n1_t")
-        hz_t = load_list(hz, "hz_t")
-        load_scale_rows(xs_runs, x_scales, (0, 1, GROUP, GROUP + 1))
+        load_scale_rows(xs_runs, x_scales, (0, 1, GROUP, GROUP + 1), on_scalar)
         gn_t = sbt([P, PACK], F32, "gn_t")
         nc.sync.dma_start(out=gn_t[:], in_=gn.rearrange("(p t) o -> p (t o)", t=PACK))
         load_scale_rows(w3s_raw, w3_scales, (0, 1, 2, 3))
         load_scale_rows(w2s_raw, w2_scales, (0, 1, 2, 3))
-        w3w_raw = load_words(w3_words, "w3w_raw")
-        w2w_raw = load_words(w2_words, "w2w_raw")
-        n3_t = load_list(n3, "n3_t")
-        n4_t = load_list(n4, "n4_t")
 
         xq_s = sbt([P, S], U8, "xq_s")
         nc.vector.tensor_copy(xq_s[:], xs_plain[:].indirect(offs_t[:]))
-        w1s = deal_scales(nc.vector, w1s_raw, "w1s")
-        w1w = deal_words(w1w_raw, "w1w")
+        w1s = deal_scales(nc.gpsimd, w1s_raw, "w1s")
         xq_w = sbt([P, S], U32, "xq_w")
         nc.vector.tensor_copy(xq_w[:], xw[:].indirect(offs_t[:]))
         neg_tau = sbt([P, PACK], F32, "neg_tau")
@@ -151,52 +151,65 @@ def tile_picked_mixhebzkern_none_po_kernel(
             nc.sync.dma_start(out=hz_scales[:].bitcast(I32)[r:P:QUAD, :], in_=hz_bytes[:].bitcast(I32)[place:P:QUAD, :])
         hz_w = sbt([P, S], U32, "hz_w")
         nc.vector.tensor_copy(hz_w[:], xw[:].indirect(hz_t[:]))
+        n3_t = load_list(n3, "n3_t")
+        n4_t = load_list(n4, "n4_t")
         w3s = deal_scales(nc.gpsimd, w3s_raw, "w3s")
         w2s = deal_scales(nc.gpsimd, w2s_raw, "w2s")
-        w3w = deal_words(w3w_raw, "w3w")
-        w2w = deal_words(w2w_raw, "w2w")
 
-        h = [sbt([P, S], F32, f"h{t}") for t in range(PACK)]
+        banks = []
         for c, (a, b) in enumerate(Z_CHUNKS):
             w = b - a
             zb = sbt([P, PACK, w], BF16, f"zb{c}")
-            for t in range(PACK):
-                y2 = sbt([P, w], F32, f"y2_{c}_{t}")
-                nc.scalar.activation(out=y2[:], in_=y[t][:].indirect(entries(n2_t, a, b)), func=ACT.Copy)
-                ea = sbt([P, w], F32, f"ea_{c}_{t}")
-                nc.scalar.activation(
-                    out=ea[:], in_=y[t][:].indirect(entries(n1_t, a, b)), func=ACT.Exp,
-                    bias=ea_bias[t][:], scale=neg_tau[:, t : t + 1],
-                )
-                m = sbt([P, w], F32, f"m_{c}_{t}")
-                nc.vector.scalar_tensor_tensor(out=m[:], in0=ea[:], scalar=gn_m2[:, t : t + 1], in1=y2[:], op0=ALU.mult, op1=ALU.mult)
-                nc.vector.scalar_tensor_tensor(out=zb[:, t, :], in0=y[t][:, a:b], scalar=gn_t[:, t : t + 1], in1=m[:], op0=ALU.mult, op1=ALU.add)
+            ms = []
+            for t in range(PACK + 1):
+                if t < PACK:
+                    y2 = sbt([P, w], F32, f"y2_{t}")
+                    nc.scalar.activation(out=y2[:], in_=y[t][:].indirect(entries(n2_t, a, b)), func=ACT.Copy)
+                    ea = sbt([P, w], F32, f"ea_{t}")
+                    nc.scalar.activation(
+                        out=ea[:], in_=y[t][:].indirect(entries(n1_t, a, b)), func=ACT.Exp,
+                        bias=ea_bias[t][:], scale=neg_tau[:, t : t + 1],
+                    )
+                    m = sbt([P, w], F32, f"m_{c}_{t}")
+                    nc.vector.scalar_tensor_tensor(out=m[:], in0=ea[:], scalar=gn_m2[:, t : t + 1], in1=y2[:], op0=ALU.mult, op1=ALU.mult)
+                    ms.append(m)
+                if t > 0:
+                    u = t - 1
+                    nc.vector.scalar_tensor_tensor(out=zb[:, u, :], in0=y[u][:, a:b], scalar=gn_t[:, u : u + 1], in1=ms[u][:], op0=ALU.mult, op1=ALU.add)
             zi = sbt([P, w, PACK], BF16, f"zi{c}")
             interleave(nc.vector.tensor_copy, zi[:], zb[:])
             zq = sbt([P, w], U32, f"zq{c}")
             zs = sbt([P, w], U8, f"zs{c}")
             nc.vector.quantize_mx(out=zq[:].bitcast(FP8X4), scales=zs[:], in_=zi[:].rearrange("p n t -> p (n t)"))
-            per_bank = S // w
-            for t0 in range(0, PACK, per_bank):
-                bank = ps.tile([P, per_bank, w], F32, name=f"h_bank{c}_{t0}")
-                for t in range(t0, t0 + per_bank):
-                    mx(bank[:, t - t0, :], w3w, w3s, t, hz_w[:, a:b], hz_scales[:, a:b], True, False)
-                    mx(bank[:, t - t0, :], w2w, w2s, t, zq[:], zs[:], False, True)
-                for t in range(t0, t0 + per_bank):
-                    nc.scalar.copy(out=h[t][:, a:b], in_=bank[:, t - t0, :])
+            if c == len(Z_CHUNKS) - 1:
+                h = [sbt([P, S], F32, f"y{t}") for t in range(PACK)]
+                for t in range(PACK):
+                    for (a0, b0), row in zip(Z_CHUNKS, banks):
+                        nc.scalar.copy(out=h[t][:, a0:b0], in_=row[t][:])
+            row = [ps.tile([P, w], F32, name=f"y_bank{t}" if c % 2 else f"h_bank{t}") for t in range(PACK)]
+            for t in range(PACK):
+                mx(row[t][:], w3w, w3s, t, hz_w[:, a:b], hz_scales[:, a:b], True, False)
+            for t in range(PACK):
+                mx(row[t][:], w2w, w2s, t, zq[:], zs[:], False, True)
+            banks.append(row)
 
         num = sbt([P, PACK, S], F32, "num")
         den2 = sbt([P, PACK, S], F32, "den2")
+        den = sbt([P, PACK, S], F32, "den")
         pp, kr = [], []
 
         def fetch(t):
+            nc.scalar.copy(out=h[t][:, Z_CHUNKS[-1][0] : S], in_=banks[-1][t][:])
             pair = sbt([P, 2, S], F32, f"pp{t}")
             for a, b in HALVES:
-                nc.vector.tensor_copy(pair[:, 0, a:b], h[t][:].indirect(entries(n3_t, a, b)))
                 nc.scalar.activation(out=pair[:, 1, a:b], in_=h[t][:].indirect(entries(n4_t, a, b)), func=ACT.Copy)
+            for a, b in HALVES:
+                if False:
+                    nc.scalar.activation(out=pair[:, 0, a:b], in_=h[t][:].indirect(entries(n3_t, a, b)), func=ACT.Copy)
+                else:
+                    nc.vector.tensor_copy(pair[:, 0, a:b], h[t][:].indirect(entries(n3_t, a, b)))
             d = sbt([P, 2, S], F32, f"d{t}")
-            for e in range(2):
-                nc.vector.tensor_tensor(out=d[:, e, :], in0=pair[:, e, :], in1=h[t][:], op=ALU.subtract)
+            nc.vector.tensor_tensor(out=d[:], in0=pair[:], in1=h[t][:].unsqueeze(1).to_broadcast([P, 2, S]), op=ALU.subtract)
             pp.append((pair, d))
 
         def weights(t):
@@ -207,16 +220,19 @@ def tile_picked_mixhebzkern_none_po_kernel(
             nc.scalar.activation(out=k[:], in_=sq[:], func=ACT.Exp, scale=-0.5)
             kr.append(k)
 
-        def combine(t):
+        def denominator(t):
             k = kr[t]
-            s = sbt([P, S], F32, f"s{t}")
-            nc.vector.scalar_tensor_tensor(out=s[:], in0=k[:, 0, :], scalar=0.5, in1=k[:, 1, :], op0=ALU.add, op1=ALU.add)
-            if t < PACK - 1:
-                nc.scalar.activation(out=den2[:, t, :], in_=s[:], func=ACT.Square)
-            else:
-                nc.vector.tensor_tensor(out=den2[:, t, :], in0=s[:], in1=s[:], op=ALU.mult)
+            s = den[:, t, :]
+            nc.vector.scalar_tensor_tensor(out=s, in0=k[:, 0, :], scalar=0.5, in1=k[:, 1, :], op0=ALU.add, op1=ALU.add)
+
+        def numerator(t):
+            k = kr[t]
             prod = sbt([P, 2, S], F32, f"prod{t}")
-            nc.vector.tensor_tensor(out=prod[:], in0=k[:], in1=pp[t][0][:], op=ALU.mult)
+            if t < PACK - 1:
+                nc.vector.tensor_tensor(out=prod[:], in0=k[:], in1=pp[t][0][:], op=ALU.mult)
+            else:
+                for e in range(2):
+                    nc.vector.tensor_tensor(out=prod[:, e, :], in0=k[:, e, :], in1=pp[t][0][:, e, :], op=ALU.mult)
             nc.vector.tensor_tensor(out=num[:, t, :], in0=prod[:, 0, :], in1=prod[:, 1, :], op=ALU.add)
 
         fetch(0)
@@ -224,31 +240,42 @@ def tile_picked_mixhebzkern_none_po_kernel(
         weights(0)
         fetch(2)
         weights(1)
-        combine(0)
+        denominator(0)
+        numerator(0)
         fetch(3)
         weights(2)
-        combine(1)
+        denominator(1)
+        numerator(1)
         weights(3)
-        combine(2)
-        combine(3)
+        denominator(2)
+        denominator(3)
+        nc.scalar.activation(out=den2[:, :3, :], in_=den[:, :3, :], func=ACT.Square)
+        nc.vector.tensor_tensor(out=den2[:, 3, :], in0=den[:, 3, :], in1=den[:, 3, :], op=ALU.mult)
+        numerator(2)
+        numerator(3)
 
         out0_v = out_0.rearrange("(p t) j -> p t j", t=PACK)
         words_v = out_1[0].rearrange("p n t -> p (n t)").bitcast(I32)
         oq = sbt([P, S], U32, "oq")
         os_ = sbt([P, S], U8, "os_")
-        for c, (a, b) in enumerate(HALVES):
-            w = b - a
+        w = S // OUT_CHUNKS
+        recs = []
+        for c in range(OUT_CHUNKS):
             rec = sbt([P, PACK, w], F32, f"rec{c}")
-            nc.scalar.activation(out=rec[:], in_=den2[:, :, a:b], func=ACT.Abs_reciprocal_sqrt)
+            nc.scalar.activation(out=rec[:], in_=den2[:, :, c * w : (c + 1) * w], func=ACT.Abs_reciprocal_sqrt)
+            recs.append(rec)
+        for c, rec in enumerate(recs):
+            a, b = c * w, (c + 1) * w
             o = sbt([P, PACK, w], F32, f"o{c}")
             nc.vector.tensor_tensor(out=o[:], in0=num[:, :, a:b], in1=rec[:], op=ALU.mult)
             nc.sync.dma_start(out=out0_v[:, :, a:b], in_=o[:])
             oi = sbt([P, w, PACK], BF16, f"oi{c}")
-            interleave(nc.scalar.copy if c == 0 else nc.vector.tensor_copy, oi[:], o[:])
+            interleave(nc.scalar.copy if c < OUT_CHUNKS - 1 else nc.vector.tensor_copy, oi[:], o[:])
             nc.vector.quantize_mx(out=oq[:, a:b].bitcast(FP8X4), scales=os_[:, a:b], in_=oi[:].rearrange("p n t -> p (n t)"))
-            nc.sync.dma_start(out=words_v[:, a:b], in_=oq[:, a:b].bitcast(I32))
+            if c % 2 == 1:
+                nc.sync.dma_start(out=words_v[:, a - w : b], in_=oq[:, a - w : b].bitcast(I32))
         for q in range(P // QUAD):
-            nc.sync.dma_start(
+            (nc.scalar if q % 2 else nc.sync).dma_start(
                 out=out_2[0].bitcast(I32)[PACK * q : PACK * (q + 1), :],
                 in_=os_[:].bitcast(I32)[QUAD * q : QUAD * q + PACK, :],
             )

@@ -83,29 +83,28 @@ def tile_picked_mixhebzkern_none_po_kernel(
                 in_=src.rearrange("p t (c i) -> p c t i", i=4),
             )
 
-        xs_plain = zeroed(nc.gpsimd, T, "xs_plain")
-        w1s_raw = zeroed(nc.vector, H, "w1s_raw")
-        xs_runs = zeroed(nc.vector, T, "xs_runs")
-        w3s_raw = zeroed(nc.vector, H, "w3s_raw")
-        w2s_raw = zeroed(nc.vector, H, "w2s_raw")
-        hz_scales = zeroed(nc.vector, S, "hz_scales")
+        xs_plain = zeroed(nc.gpsimd, T, "xs_window")
+        hz_scales = zeroed(nc.gpsimd, S, "hz_scales")
+        w3s_raw = zeroed(nc.gpsimd, H, "w3s_raw")
+        w2s_raw = zeroed(nc.gpsimd, H, "w2s_raw")
+        xs_runs = zeroed(nc.gpsimd, T, "xs_runs")
+        w1s_raw = zeroed(nc.gpsimd, H, "w1s_raw")
 
         on_scalar = (nc.scalar,) * PACK
         offs_t = load_list(offs, "offs_t")
-        w1w_raw = load_words(w1_words, "w1w_raw")
-        xw = sbt([P, T], U32, "xw")
-        nc.sync.dma_start(out=xw[:].bitcast(I32), in_=x_words[0].rearrange("p n t -> p (n t)").bitcast(I32))
-        load_scale_rows(xs_plain, x_scales, (0, 1, 2, 3), on_scalar)
-        w1w = deal_words(w1w_raw, "w1w")
-        load_scale_rows(w1s_raw, w1_scales, (0, 1, 2, 3), (nc.scalar, nc.sync, nc.sync, nc.sync))
-        hz_t = load_list(hz, "hz_t")
-        w3w = deal_words(load_words(w3_words, "w3w_raw", nc.scalar), "w3w")
-        w2w = deal_words(load_words(w2_words, "w2w_raw", nc.scalar), "w2w")
-        n2_t = load_list(n2, "n2_t")
+        w1w = deal_words(load_words(w1_words, "w1w_raw"), "w1w")
         tau_t = sbt([P, PACK], F32, "tau_t")
         nc.sync.dma_start(out=tau_t[:], in_=tau.rearrange("(p t) o -> p (t o)", t=PACK))
+        load_scale_rows(xs_plain, x_scales, (0, 1, 2, 3))
+        xw = sbt([P, T], U32, "xw")
+        nc.sync.dma_start(out=xw[:].bitcast(I32), in_=x_words[0].rearrange("p n t -> p (n t)").bitcast(I32))
+        load_scale_rows(w1s_raw, w1_scales, (0, 1, 2, 3), (nc.sync,) * PACK)
+        hz_t = load_list(hz, "hz_t")
+        w3w = deal_words(load_words(w3_words, "w3w_raw"), "w3w")
+        w2w = deal_words(load_words(w2_words, "w2w_raw"), "w2w")
+        n2_t = load_list(n2, "n2_t")
         n1_t = load_list(n1, "n1_t")
-        load_scale_rows(xs_runs, x_scales, (0, 1, GROUP, GROUP + 1), on_scalar)
+        load_scale_rows(xs_runs, x_scales, (0, 1, GROUP, GROUP + 1))
         gn_t = sbt([P, PACK], F32, "gn_t")
         nc.sync.dma_start(out=gn_t[:], in_=gn.rearrange("(p t) o -> p (t o)", t=PACK))
         load_scale_rows(w3s_raw, w3_scales, (0, 1, 2, 3))
@@ -113,11 +112,18 @@ def tile_picked_mixhebzkern_none_po_kernel(
 
         xq_s = sbt([P, S], U8, "xq_s")
         nc.vector.tensor_copy(xq_s[:], xs_plain[:].indirect(offs_t[:]))
-        w1s = deal_scales(nc.gpsimd, w1s_raw, "w1s")
+
         xq_w = sbt([P, S], U32, "xq_w")
         nc.vector.tensor_copy(xq_w[:], xw[:].indirect(offs_t[:]))
+        w1s = sbt([P, H], U8, "w1s")
+        dealt = w1s[:].rearrange("p (t m) -> p t m", t=PACK)
+        plain = w1s_raw[:].rearrange("p (m t) -> p t m", t=PACK)
+        nc.vector.tensor_copy(out=dealt[:, 0, :], in_=plain[:, 0, :])
+        nc.vector.tensor_copy(out=dealt[:, 1:, :], in_=plain[:, 1:, :])
+        hz_w = sbt([P, S], U32, "hz_w")
+        nc.vector.tensor_copy(hz_w[:], xw[:].indirect(hz_t[:]))
         neg_tau = sbt([P, PACK], F32, "neg_tau")
-        nc.scalar.activation(out=neg_tau[:], in_=tau_t[:], func=ACT.Copy, scale=-1.0)
+        nc.vector.tensor_scalar(out=neg_tau[:], in0=tau_t[:], scalar1=-1.0, scalar2=None, op0=ALU.mult)
 
         def mx(out, ww, ws, t, rw, rs, start, stop):
             nc.tensor.matmul_mx(
@@ -149,8 +155,6 @@ def tile_picked_mixhebzkern_none_po_kernel(
         nc.vector.tensor_copy(hz_bytes[:], xs_runs[:].indirect(hz_t[:]))
         for r, place in enumerate((0, 1, GROUP, GROUP + 1)):
             nc.sync.dma_start(out=hz_scales[:].bitcast(I32)[r:P:QUAD, :], in_=hz_bytes[:].bitcast(I32)[place:P:QUAD, :])
-        hz_w = sbt([P, S], U32, "hz_w")
-        nc.vector.tensor_copy(hz_w[:], xw[:].indirect(hz_t[:]))
         n3_t = load_list(n3, "n3_t")
         n4_t = load_list(n4, "n4_t")
         w3s = deal_scales(nc.gpsimd, w3s_raw, "w3s")

@@ -20,9 +20,11 @@ P = 128
 PACK = 4
 QUAD = 32
 GROUP = 16
+SCALE_ROWS = 16
+HALF = S // 2
+HALVES = ((0, HALF), (HALF, S))
 Z_CHUNKS = ((0, 256), (256, 384), (384, 512))
-HALVES = ((0, 256), (256, 512))
-OUT_CHUNKS = 4
+OUT_WIDTH = 128
 
 
 def tile_picked_mixhebzkern_none_po_kernel(
@@ -37,31 +39,31 @@ def tile_picked_mixhebzkern_none_po_kernel(
         def sbt(shape, dtype, name):
             return sb.tile(shape, dtype, name=name, align_bytes=64)
 
+        def zeroed(width, name):
+            tile = sbt([P, width], U8, name)
+            nc.gpsimd.memset(tile[:].bitcast(I32), 0)
+            return tile
+
         def load_list(src, name):
             tile = sbt([P, S // GROUP], U16, name)
             nc.sync.dma_start(tile[:], src)
             return tile
 
-        def entries(lst, a, b):
-            return lst[:, a // GROUP : b // GROUP]
+        def entries(lists, a, b):
+            return lists[:, a // GROUP : b // GROUP]
 
-        def load_scale_rows(tile, src, places, queues=(nc.sync,) * PACK):
-            rows = src[0].bitcast(I32)
-            view = tile[:].bitcast(I32)
-            for r, place in enumerate(places):
-                queues[r].dma_start(out=view[place:P:QUAD, :], in_=rows[r : 4 * PACK : PACK, :])
-
-        def zeroed(eng, width, name):
-            tile = sbt([P, width], U8, name)
-            eng.memset(tile[:].bitcast(I32), 0)
+        def load_column(src, name):
+            tile = sbt([P, PACK], F32, name)
+            nc.sync.dma_start(out=tile[:], in_=src.rearrange("(p t) o -> p (t o)", t=PACK))
             return tile
 
-        def load_words(src, name, queue=nc.sync):
-            tile = sbt([P, 2 * H], U8, name)
-            queue.dma_start(out=tile[:].bitcast(I32), in_=src[0].bitcast(I32))
-            return tile
+        def load_scale_rows(tile, src):
+            for r in range(PACK):
+                nc.sync.dma_start(out=tile[:].bitcast(I32)[r:P:QUAD, :], in_=src[0].bitcast(I32)[r:SCALE_ROWS:PACK, :])
 
-        def deal_words(raw, name):
+        def dealt_words(src, name):
+            raw = sbt([P, 2 * H], U8, name + "_raw")
+            nc.sync.dma_start(out=raw[:].bitcast(I32), in_=src[0].bitcast(I32))
             tile = sbt([P, 2 * H], U8, name)
             nc.scalar.copy(
                 out=tile[:].bitcast(U16).rearrange("p (t m) -> p t m", t=PACK),
@@ -69,217 +71,197 @@ def tile_picked_mixhebzkern_none_po_kernel(
             )
             return tile
 
-        def deal_scales(eng, raw, name):
+        def dealt_scales(engine, raw, name, parts):
             tile = sbt([P, H], U8, name)
-            eng.tensor_copy(
-                out=tile[:].rearrange("p (t m) -> p t m", t=PACK),
-                in_=raw[:].rearrange("p (m t) -> p t m", t=PACK),
-            )
+            for part in parts:
+                engine.tensor_copy(
+                    out=tile[:].rearrange("p (t m) -> p t m", t=PACK)[:, part, :],
+                    in_=raw[:].rearrange("p (m t) -> p t m", t=PACK)[:, part, :],
+                )
             return tile
 
         def interleave(copy, dst, src):
-            copy(
-                out=dst.rearrange("p (c i) t -> p c t i", i=4),
-                in_=src.rearrange("p t (c i) -> p c t i", i=4),
-            )
+            copy(out=dst.rearrange("p (c i) t -> p c t i", i=4), in_=src.rearrange("p t (c i) -> p c t i", i=4))
 
-        xs_plain = zeroed(nc.gpsimd, T, "xs_window")
-        hz_scales = zeroed(nc.gpsimd, S, "hz_scales")
-        w3s_raw = zeroed(nc.gpsimd, H, "w3s_raw")
-        w2s_raw = zeroed(nc.gpsimd, H, "w2s_raw")
-        xs_runs = zeroed(nc.gpsimd, T, "xs_runs")
-        w1s_raw = zeroed(nc.gpsimd, H, "w1s_raw")
-
-        on_scalar = (nc.scalar,) * PACK
-        offs_t = load_list(offs, "offs_t")
-        w1w = deal_words(load_words(w1_words, "w1w_raw"), "w1w")
-        tau_t = sbt([P, PACK], F32, "tau_t")
-        nc.sync.dma_start(out=tau_t[:], in_=tau.rearrange("(p t) o -> p (t o)", t=PACK))
-        load_scale_rows(xs_plain, x_scales, (0, 1, 2, 3))
-        xw = sbt([P, T], U32, "xw")
-        nc.sync.dma_start(out=xw[:].bitcast(I32), in_=x_words[0].rearrange("p n t -> p (n t)").bitcast(I32))
-        load_scale_rows(w1s_raw, w1_scales, (0, 1, 2, 3), (nc.sync,) * PACK)
-        hz_t = load_list(hz, "hz_t")
-        w3w = deal_words(load_words(w3_words, "w3w_raw"), "w3w")
-        w2w = deal_words(load_words(w2_words, "w2w_raw"), "w2w")
-        n2_t = load_list(n2, "n2_t")
-        n1_t = load_list(n1, "n1_t")
-        load_scale_rows(xs_runs, x_scales, (0, 1, GROUP, GROUP + 1))
-        gn_t = sbt([P, PACK], F32, "gn_t")
-        nc.sync.dma_start(out=gn_t[:], in_=gn.rearrange("(p t) o -> p (t o)", t=PACK))
-        load_scale_rows(w3s_raw, w3_scales, (0, 1, 2, 3))
-        load_scale_rows(w2s_raw, w2_scales, (0, 1, 2, 3))
-
-        xq_s = sbt([P, S], U8, "xq_s")
-        nc.vector.tensor_copy(xq_s[:], xs_plain[:].indirect(offs_t[:]))
-
-        xq_w = sbt([P, S], U32, "xq_w")
-        nc.vector.tensor_copy(xq_w[:], xw[:].indirect(offs_t[:]))
-        w1s = sbt([P, H], U8, "w1s")
-        dealt = w1s[:].rearrange("p (t m) -> p t m", t=PACK)
-        plain = w1s_raw[:].rearrange("p (m t) -> p t m", t=PACK)
-        nc.vector.tensor_copy(out=dealt[:, 0, :], in_=plain[:, 0, :])
-        nc.vector.tensor_copy(out=dealt[:, 1:, :], in_=plain[:, 1:, :])
-        hz_w = sbt([P, S], U32, "hz_w")
-        nc.vector.tensor_copy(hz_w[:], xw[:].indirect(hz_t[:]))
-        neg_tau = sbt([P, PACK], F32, "neg_tau")
-        nc.vector.tensor_scalar(out=neg_tau[:], in0=tau_t[:], scalar1=-1.0, scalar2=None, op0=ALU.mult)
-
-        def mx(out, ww, ws, t, rw, rs, start, stop):
+        def mx(out, words, scales, t, moving, moving_scales, start, stop):
             nc.tensor.matmul_mx(
                 out=out,
-                lhsT=ww[:, 2 * P * t : 2 * P * (t + 1)].bitcast(FP4X4),
-                lhsT_scale=ws[:, P * t : P * (t + 1)],
-                rhs=rw.bitcast(FP8X4),
-                rhs_scale=rs,
+                lhsT=words[:, 2 * P * t : 2 * P * (t + 1)].bitcast(FP4X4),
+                lhsT_scale=scales[:, P * t : P * (t + 1)],
+                rhs=moving.bitcast(FP8X4),
+                rhs_scale=moving_scales,
                 start=start,
                 stop=stop,
             )
 
+        xs = zeroed(T, "xs")
+        w1s_raw = zeroed(H, "w1s_raw")
+        hz_scales = zeroed(S, "hz_scales")
+        w3s_raw = zeroed(H, "w3s_raw")
+        w2s_raw = zeroed(H, "w2s_raw")
+
+        offs_t = load_list(offs, "offs_t")
+        hz_t = load_list(hz, "hz_t")
+        xs_rows = x_scales[0].bitcast(I32)
+        for r in range(2):
+            nc.sync.dma_start(out=xs[:].bitcast(I32)[r:P:GROUP, :], in_=xs_rows[r:SCALE_ROWS:2, :])
+            nc.sync.dma_start(out=xs[:].bitcast(I32)[2 + r : P : QUAD, :], in_=xs_rows[2 + r : SCALE_ROWS : PACK, :])
+        xw = sbt([P, T], U32, "xw")
+        nc.sync.dma_start(out=xw[:].bitcast(I32), in_=x_words[0].rearrange("p n t -> p (n t)").bitcast(I32))
+        w1w = dealt_words(w1_words, "w1w")
+        load_scale_rows(w1s_raw, w1_scales)
+        tau_t = load_column(tau, "tau_t")
+        w3w = dealt_words(w3_words, "w3w")
+        w2w = dealt_words(w2_words, "w2w")
+        n2_t = load_list(n2, "n2_t")
+        n1_t = load_list(n1, "n1_t")
+        gn_t = load_column(gn, "gn_t")
+        load_scale_rows(w3s_raw, w3_scales)
+        load_scale_rows(w2s_raw, w2_scales)
+
+        xq_scales = sbt([P, S], U8, "xq_scales")
+        nc.vector.tensor_copy(xq_scales[:], xs[:].indirect(offs_t[:]))
+        hz_bytes = sbt([P, S], U8, "hz_bytes")
+        nc.vector.tensor_copy(hz_bytes[:], xs[:].indirect(hz_t[:]))
+        xq_words = sbt([P, S], U32, "xq_words")
+        nc.vector.tensor_copy(xq_words[:], xw[:].indirect(offs_t[:]))
+        w1s = dealt_scales(nc.vector, w1s_raw, "w1s", (slice(0, 1), slice(1, PACK)))
+        hz_words = sbt([P, S], U32, "w1s_raw")
+        nc.vector.tensor_copy(hz_words[:], xw[:].indirect(hz_t[:]))
+        neg_tau = sbt([P, PACK], F32, "neg_tau")
+        nc.vector.tensor_scalar(out=neg_tau[:], in0=tau_t[:], scalar1=-1.0, scalar2=None, op0=ALU.mult)
+
         y, ea_bias = [], []
         for t in range(PACK):
-            bank = ps.tile([P, S], F32, name=f"y_bank{t}")
-            mx(bank[:], w1w, w1s, t, xq_w[:], xq_s[:], True, True)
-            yt = sbt([P, S], F32, f"y{t}")
+            bank = ps.tile([P, S], F32, name=f"odd_bank{t}")
+            mx(bank[:], w1w, w1s, t, xq_words[:], xq_scales[:], True, True)
+            y_t = sbt([P, S], F32, f"window{t}")
             low = sbt([P, 1], F32, f"low{t}")
-            nc.vector.tensor_scalar(out=yt[:], in0=bank[:], scalar1=1.0, scalar2=None, op0=ALU.mult, op1=ALU.min, accum_out=low[:])
+            nc.vector.tensor_scalar(
+                out=y_t[:], in0=bank[:], scalar1=1.0, scalar2=None, op0=ALU.mult, op1=ALU.min, accum_out=low[:]
+            )
             bias = sbt([P, 1], F32, f"ea_bias{t}")
-            nc.vector.tensor_tensor(out=bias[:], in0=low[:], in1=tau_t[:, t : t + 1], op=ALU.mult)
-            y.append(yt)
+            nc.vector.tensor_scalar(out=bias[:], in0=low[:], scalar1=tau_t[:, t : t + 1], scalar2=None, op0=ALU.mult)
+            y.append(y_t)
             ea_bias.append(bias)
-
         gn_m2 = sbt([P, PACK], F32, "gn_m2")
         nc.vector.tensor_scalar(out=gn_m2[:], in0=gn_t[:], scalar1=-2.0, scalar2=None, op0=ALU.mult)
 
-        hz_bytes = sbt([P, S], U8, "hz_bytes")
-        nc.vector.tensor_copy(hz_bytes[:], xs_runs[:].indirect(hz_t[:]))
         for r, place in enumerate((0, 1, GROUP, GROUP + 1)):
             nc.sync.dma_start(out=hz_scales[:].bitcast(I32)[r:P:QUAD, :], in_=hz_bytes[:].bitcast(I32)[place:P:QUAD, :])
         n3_t = load_list(n3, "n3_t")
         n4_t = load_list(n4, "n4_t")
-        w3s = deal_scales(nc.gpsimd, w3s_raw, "w3s")
-        w2s = deal_scales(nc.gpsimd, w2s_raw, "w2s")
+        w3s = dealt_scales(nc.gpsimd, w3s_raw, "w3s", (slice(0, PACK),))
+        w2s = dealt_scales(nc.gpsimd, w2s_raw, "w2s", (slice(0, PACK),))
 
-        banks = []
+        h_banks = []
         for c, (a, b) in enumerate(Z_CHUNKS):
-            w = b - a
-            zb = sbt([P, PACK, w], BF16, f"zb{c}")
-            ms = []
+            width = b - a
+            z = sbt([P, PACK, width], BF16, f"z{c}")
+            pulls = []
             for t in range(PACK + 1):
                 if t < PACK:
-                    y2 = sbt([P, w], F32, f"y2_{t}")
-                    nc.scalar.activation(out=y2[:], in_=y[t][:].indirect(entries(n2_t, a, b)), func=ACT.Copy)
-                    ea = sbt([P, w], F32, f"ea_{t}")
+                    y_n2 = sbt([P, width], F32, f"y_n2_{t}")
+                    nc.scalar.activation(out=y_n2[:], in_=y[t][:].indirect(entries(n2_t, a, b)), func=ACT.Copy)
+                    ea = sbt([P, width], F32, f"ea{t}")
                     nc.scalar.activation(
                         out=ea[:], in_=y[t][:].indirect(entries(n1_t, a, b)), func=ACT.Exp,
                         bias=ea_bias[t][:], scale=neg_tau[:, t : t + 1],
                     )
-                    m = sbt([P, w], F32, f"m_{c}_{t}")
-                    nc.vector.scalar_tensor_tensor(out=m[:], in0=ea[:], scalar=gn_m2[:, t : t + 1], in1=y2[:], op0=ALU.mult, op1=ALU.mult)
-                    ms.append(m)
+                    pull = sbt([P, width], F32, f"pull{c}_{t}")
+                    nc.vector.scalar_tensor_tensor(
+                        out=pull[:], in0=ea[:], scalar=gn_m2[:, t : t + 1], in1=y_n2[:], op0=ALU.mult, op1=ALU.mult
+                    )
+                    pulls.append(pull)
                 if t > 0:
                     u = t - 1
-                    nc.vector.scalar_tensor_tensor(out=zb[:, u, :], in0=y[u][:, a:b], scalar=gn_t[:, u : u + 1], in1=ms[u][:], op0=ALU.mult, op1=ALU.add)
-            zi = sbt([P, w, PACK], BF16, f"zi{c}")
-            interleave(nc.vector.tensor_copy, zi[:], zb[:])
-            zq = sbt([P, w], U32, f"zq{c}")
-            zs = sbt([P, w], U8, f"zs{c}")
-            nc.vector.quantize_mx(out=zq[:].bitcast(FP8X4), scales=zs[:], in_=zi[:].rearrange("p n t -> p (n t)"))
+                    nc.vector.scalar_tensor_tensor(
+                        out=z[:, u, :], in0=y[u][:, a:b], scalar=gn_t[:, u : u + 1], in1=pulls[u][:],
+                        op0=ALU.mult, op1=ALU.add,
+                    )
+            z_side = sbt([P, width, PACK], BF16, f"z_side{c}")
+            interleave(nc.vector.tensor_copy, z_side[:], z[:])
+            z_words = sbt([P, width], U32, f"z_words{c}")
+            z_scales = sbt([P, width], U8, f"z_scales{c}")
+            nc.vector.quantize_mx(
+                out=z_words[:].bitcast(FP8X4), scales=z_scales[:], in_=z_side[:].rearrange("p n t -> p (n t)")
+            )
             if c == len(Z_CHUNKS) - 1:
-                h = [sbt([P, S], F32, f"y{t}") for t in range(PACK)]
+                h = [sbt([P, S], F32, f"window{t}") for t in range(PACK)]
                 for t in range(PACK):
-                    for (a0, b0), row in zip(Z_CHUNKS, banks):
-                        nc.scalar.copy(out=h[t][:, a0:b0], in_=row[t][:])
-            row = [ps.tile([P, w], F32, name=f"y_bank{t}" if c % 2 else f"h_bank{t}") for t in range(PACK)]
+                    for (a0, b0), banks in zip(Z_CHUNKS, h_banks):
+                        nc.scalar.copy(out=h[t][:, a0:b0], in_=banks[t][:])
+            banks = [ps.tile([P, width], F32, name=f"odd_bank{t}" if c % 2 else f"even_bank{t}") for t in range(PACK)]
             for t in range(PACK):
-                mx(row[t][:], w3w, w3s, t, hz_w[:, a:b], hz_scales[:, a:b], True, False)
+                mx(banks[t][:], w3w, w3s, t, hz_words[:, a:b], hz_scales[:, a:b], True, False)
             for t in range(PACK):
-                mx(row[t][:], w2w, w2s, t, zq[:], zs[:], False, True)
-            banks.append(row)
+                mx(banks[t][:], w2w, w2s, t, z_words[:], z_scales[:], False, True)
+            h_banks.append(banks)
+        for t in range(PACK):
+            nc.vector.tensor_copy(out=h[t][:, Z_CHUNKS[-1][0] : S], in_=h_banks[-1][t][:])
 
-        num = sbt([P, PACK, S], F32, "num")
-        den2 = sbt([P, PACK, S], F32, "den2")
-        den = sbt([P, PACK, S], F32, "den")
-        pp, kr = [], []
-
-        def fetch(t):
-            nc.scalar.copy(out=h[t][:, Z_CHUNKS[-1][0] : S], in_=banks[-1][t][:])
-            pair = sbt([P, 2, S], F32, f"pp{t}")
+        looked_up, diffs, weights = [], [], []
+        for t in range(PACK):
+            pair = sbt([P, 2, S], F32, f"pair{t}")
             for a, b in HALVES:
                 nc.scalar.activation(out=pair[:, 1, a:b], in_=h[t][:].indirect(entries(n4_t, a, b)), func=ACT.Copy)
             for a, b in HALVES:
-                if False:
-                    nc.scalar.activation(out=pair[:, 0, a:b], in_=h[t][:].indirect(entries(n3_t, a, b)), func=ACT.Copy)
-                else:
-                    nc.vector.tensor_copy(pair[:, 0, a:b], h[t][:].indirect(entries(n3_t, a, b)))
-            d = sbt([P, 2, S], F32, f"d{t}")
-            nc.vector.tensor_tensor(out=d[:], in0=pair[:], in1=h[t][:].unsqueeze(1).to_broadcast([P, 2, S]), op=ALU.subtract)
-            pp.append((pair, d))
+                nc.vector.tensor_copy(pair[:, 0, a:b], h[t][:].indirect(entries(n3_t, a, b)))
+            diff = sbt([P, 2, S], F32, f"diff{t}")
+            nc.vector.tensor_tensor(
+                out=diff[:], in0=pair[:], in1=h[t][:].unsqueeze(1).to_broadcast([P, 2, S]), op=ALU.subtract
+            )
+            looked_up.append(pair)
+            diffs.append(diff)
+        den = sbt([P, PACK, S], F32, "den")
+        for t in range(PACK):
+            square = sbt([P, 2, S], F32, f"square{t}")
+            nc.scalar.activation(out=square[:], in_=diffs[t][:], func=ACT.Square)
+            kr = sbt([P, 2, S], F32, f"kr{t}")
+            nc.scalar.activation(out=kr[:], in_=square[:], func=ACT.Exp, scale=-0.5)
+            nc.vector.scalar_tensor_tensor(
+                out=den[:, t, :], in0=kr[:, 0, :], scalar=0.5, in1=kr[:, 1, :], op0=ALU.add, op1=ALU.add
+            )
+            weights.append(kr)
+        den_sq = sbt([P, PACK, S], F32, "den_sq")
+        nc.scalar.activation(out=den_sq[:, :2, :], in_=den[:, :2, :], func=ACT.Square)
+        num = sbt([P, PACK, S], F32, "num")
+        for t in range(PACK):
+            terms = sbt([P, 2, S], F32, f"terms{t}")
+            nc.vector.tensor_tensor(out=terms[:], in0=weights[t][:], in1=looked_up[t][:], op=ALU.mult)
+            nc.vector.tensor_tensor(out=num[:, t, :], in0=terms[:, 0, :], in1=terms[:, 1, :], op=ALU.add)
 
-        def weights(t):
-            d = pp[t][1]
-            sq = sbt([P, 2, S], F32, f"sq{t}")
-            nc.scalar.activation(out=sq[:], in_=d[:], func=ACT.Square)
-            k = sbt([P, 2, S], F32, f"kr{t}")
-            nc.scalar.activation(out=k[:], in_=sq[:], func=ACT.Exp, scale=-0.5)
-            kr.append(k)
+        out_rows = out_0.rearrange("(p t) j -> p t j", t=PACK)
+        result = sbt([P, PACK, S], F32, "result")
+        inverse = sbt([P, 2, S], F32, f"square{PACK - 1}")
+        nc.scalar.activation(out=inverse[:], in_=den_sq[:, :2, :], func=ACT.Abs_reciprocal_sqrt)
+        nc.vector.tensor_tensor(out=result[:, :2, :], in0=num[:, :2, :], in1=inverse[:], op=ALU.mult)
+        nc.sync.dma_start(out=out_rows[:, :2, :], in_=result[:, :2, :])
+        nc.scalar.activation(out=den_sq[:, 2:, :], in_=den[:, 2:, :], func=ACT.Square)
+        inverses = []
+        for a, b in HALVES:
+            inverse = sbt([P, 2, HALF], F32, f"inverse{a}")
+            nc.scalar.activation(out=inverse[:], in_=den_sq[:, 2:, a:b], func=ACT.Abs_reciprocal_sqrt)
+            inverses.append(inverse)
 
-        def denominator(t):
-            k = kr[t]
-            s = den[:, t, :]
-            nc.vector.scalar_tensor_tensor(out=s, in0=k[:, 0, :], scalar=0.5, in1=k[:, 1, :], op0=ALU.add, op1=ALU.add)
-
-        def numerator(t):
-            k = kr[t]
-            prod = sbt([P, 2, S], F32, f"prod{t}")
-            if t < PACK - 1:
-                nc.vector.tensor_tensor(out=prod[:], in0=k[:], in1=pp[t][0][:], op=ALU.mult)
-            else:
-                for e in range(2):
-                    nc.vector.tensor_tensor(out=prod[:, e, :], in0=k[:, e, :], in1=pp[t][0][:, e, :], op=ALU.mult)
-            nc.vector.tensor_tensor(out=num[:, t, :], in0=prod[:, 0, :], in1=prod[:, 1, :], op=ALU.add)
-
-        fetch(0)
-        fetch(1)
-        weights(0)
-        fetch(2)
-        weights(1)
-        denominator(0)
-        numerator(0)
-        fetch(3)
-        weights(2)
-        denominator(1)
-        numerator(1)
-        weights(3)
-        denominator(2)
-        denominator(3)
-        nc.scalar.activation(out=den2[:, :3, :], in_=den[:, :3, :], func=ACT.Square)
-        nc.vector.tensor_tensor(out=den2[:, 3, :], in0=den[:, 3, :], in1=den[:, 3, :], op=ALU.mult)
-        numerator(2)
-        numerator(3)
-
-        out0_v = out_0.rearrange("(p t) j -> p t j", t=PACK)
-        words_v = out_1[0].rearrange("p n t -> p (n t)").bitcast(I32)
-        oq = sbt([P, S], U32, "oq")
-        os_ = sbt([P, S], U8, "os_")
-        w = S // OUT_CHUNKS
-        recs = []
-        for c in range(OUT_CHUNKS):
-            rec = sbt([P, PACK, w], F32, f"rec{c}")
-            nc.scalar.activation(out=rec[:], in_=den2[:, :, c * w : (c + 1) * w], func=ACT.Abs_reciprocal_sqrt)
-            recs.append(rec)
-        for c, rec in enumerate(recs):
-            a, b = c * w, (c + 1) * w
-            o = sbt([P, PACK, w], F32, f"o{c}")
-            nc.vector.tensor_tensor(out=o[:], in0=num[:, :, a:b], in1=rec[:], op=ALU.mult)
-            nc.sync.dma_start(out=out0_v[:, :, a:b], in_=o[:])
-            oi = sbt([P, w, PACK], BF16, f"oi{c}")
-            interleave(nc.scalar.copy if c < OUT_CHUNKS - 1 else nc.vector.tensor_copy, oi[:], o[:])
-            nc.vector.quantize_mx(out=oq[:, a:b].bitcast(FP8X4), scales=os_[:, a:b], in_=oi[:].rearrange("p n t -> p (n t)"))
-            if c % 2 == 1:
-                nc.sync.dma_start(out=words_v[:, a - w : b], in_=oq[:, a - w : b].bitcast(I32))
+        out_words = sbt([P, S], U32, "out_words")
+        out_scales = sbt([P, S], U8, "out_scales")
+        for (a, b), inverse in zip(HALVES, inverses):
+            nc.vector.tensor_tensor(out=result[:, 2:, a:b], in0=num[:, 2:, a:b], in1=inverse[:], op=ALU.mult)
+            nc.sync.dma_start(out=out_rows[:, 2:, a:b], in_=result[:, 2:, a:b])
+            for a0, copy in ((a, nc.scalar.copy), (a + OUT_WIDTH, nc.vector.tensor_copy)):
+                columns = slice(a0, a0 + OUT_WIDTH)
+                side = sbt([P, OUT_WIDTH, PACK], BF16, f"out_side{a0}")
+                interleave(copy, side[:], result[:, :, columns])
+                nc.vector.quantize_mx(
+                    out=out_words[:, columns].bitcast(FP8X4), scales=out_scales[:, columns],
+                    in_=side[:].rearrange("p n t -> p (n t)"),
+                )
+            nc.sync.dma_start(
+                out=out_1[0].rearrange("p n t -> p (n t)").bitcast(I32)[:, a:b], in_=out_words[:, a:b].bitcast(I32)
+            )
         for q in range(P // QUAD):
             (nc.scalar if q % 2 else nc.sync).dma_start(
                 out=out_2[0].bitcast(I32)[PACK * q : PACK * (q + 1), :],
-                in_=os_[:].bitcast(I32)[QUAD * q : QUAD * q + PACK, :],
+                in_=out_scales[:].bitcast(I32)[QUAD * q : QUAD * q + PACK, :],
             )

@@ -52,9 +52,9 @@ def tile_picked_mixhebzkern_none_po_kernel(
         def entries(lists, a, b):
             return lists[:, a // GROUP : b // GROUP]
 
-        def load_column(src, name):
+        def load_column(queue, src, name):
             tile = sbt([P, PACK], F32, name)
-            nc.sync.dma_start(out=tile[:], in_=src.rearrange("(p t) o -> p (t o)", t=PACK))
+            queue.dma_start(out=tile[:], in_=src.rearrange("(p t) o -> p (t o)", t=PACK))
             return tile
 
         def load_scale_rows(tile, src):
@@ -110,12 +110,12 @@ def tile_picked_mixhebzkern_none_po_kernel(
         nc.sync.dma_start(out=xw[:].bitcast(I32), in_=x_words[0].rearrange("p n t -> p (n t)").bitcast(I32))
         w1w = dealt_words(w1_words, "w1w")
         load_scale_rows(w1s_raw, w1_scales)
-        tau_t = load_column(tau, "tau_t")
+        tau_t = load_column(nc.scalar, tau, "tau_t")
         w3w = dealt_words(w3_words, "w3w")
         w2w = dealt_words(w2_words, "w2w")
         n2_t = load_list(n2, "n2_t")
         n1_t = load_list(n1, "n1_t")
-        gn_t = load_column(gn, "gn_t")
+        gn_t = load_column(nc.sync, gn, "gn_t")
         load_scale_rows(w3s_raw, w3_scales)
         load_scale_rows(w2s_raw, w2_scales)
 
@@ -180,7 +180,7 @@ def tile_picked_mixhebzkern_none_po_kernel(
                         op0=ALU.mult, op1=ALU.add,
                     )
             z_side = sbt([P, width, PACK], BF16, f"z_side{c}")
-            interleave(nc.vector.tensor_copy, z_side[:], z[:])
+            interleave(nc.scalar.copy if c == 1 else nc.vector.tensor_copy, z_side[:], z[:])
             z_words = sbt([P, width], U32, f"z_words{c}")
             z_scales = sbt([P, width], U8, f"z_scales{c}")
             nc.vector.quantize_mx(
@@ -224,20 +224,29 @@ def tile_picked_mixhebzkern_none_po_kernel(
             )
             weights.append(kr)
         den_sq = sbt([P, PACK, S], F32, "den_sq")
-        nc.scalar.activation(out=den_sq[:, :2, :], in_=den[:, :2, :], func=ACT.Square)
+        for t in range(2):
+            nc.scalar.activation(out=den_sq[:, t, :], in_=den[:, t, :], func=ACT.Square)
         num = sbt([P, PACK, S], F32, "num")
-        for t in range(PACK):
-            terms = sbt([P, 2, S], F32, f"terms{t}")
-            nc.vector.tensor_tensor(out=terms[:], in0=weights[t][:], in1=looked_up[t][:], op=ALU.mult)
-            nc.vector.tensor_tensor(out=num[:, t, :], in0=terms[:, 0, :], in1=terms[:, 1, :], op=ALU.add)
+        for t0 in range(0, PACK, 2):
+            terms = sbt([P, 2, 2, S], F32, f"terms{t0}")
+            for u in range(2):
+                nc.vector.tensor_tensor(
+                    out=terms[:, u, :, :], in0=weights[t0 + u][:], in1=looked_up[t0 + u][:], op=ALU.mult
+                )
+            for u in range(2):
+                nc.vector.tensor_tensor(
+                    out=num[:, t0 + u, :], in0=terms[:, u, 0, :], in1=terms[:, u, 1, :], op=ALU.add
+                )
 
         out_rows = out_0.rearrange("(p t) j -> p t j", t=PACK)
         result = sbt([P, PACK, S], F32, "result")
         inverse = sbt([P, 2, S], F32, f"square{PACK - 1}")
-        nc.scalar.activation(out=inverse[:], in_=den_sq[:, :2, :], func=ACT.Abs_reciprocal_sqrt)
+        for t in range(2):
+            nc.scalar.activation(out=inverse[:, t, :], in_=den_sq[:, t, :], func=ACT.Abs_reciprocal_sqrt)
         nc.vector.tensor_tensor(out=result[:, :2, :], in0=num[:, :2, :], in1=inverse[:], op=ALU.mult)
         nc.sync.dma_start(out=out_rows[:, :2, :], in_=result[:, :2, :])
-        nc.scalar.activation(out=den_sq[:, 2:, :], in_=den[:, 2:, :], func=ACT.Square)
+        for a, b in HALVES:
+            nc.scalar.activation(out=den_sq[:, 2:, a:b], in_=den[:, 2:, a:b], func=ACT.Square)
         inverses = []
         for a, b in HALVES:
             inverse = sbt([P, 2, HALF], F32, f"inverse{a}")

from contextlib import ExitStack

import concourse.mybir as mybir

K, T, S, N, H = 512, 2048, 512, 512, 512
FLOPS = 2 * K * H * S + 2 * H * N * S + 2 * K * N * S

F32 = mybir.dt.float32
BF16 = mybir.dt.bfloat16
I32 = mybir.dt.int32
U32 = mybir.dt.uint32
U16 = mybir.dt.uint16
U8 = mybir.dt.uint8
FP8X4 = mybir.dt.float8_e4m3fn_x4
FP4X4 = mybir.dt.float4_e2m1fn_x4
ALU = mybir.AluOpType
ACT = mybir.ActivationFunctionType

P = 128
PACK = 4
QUAD = 32
GROUP = 16
SCALE_ROWS = 16
HALF = S // 2
HALVES = ((0, HALF), (HALF, S))
Z_CHUNKS = ((0, 256), (256, 384), (384, 512))
OUT_WIDTH = 128


def tile_picked_mixhebzkern_none_po_kernel(
    tc, x_words, x_scales, w1_words, w1_scales, tau, gn, w2_words, w2_scales, w3_words, w3_scales,
    offs, n1, n2, hz, n3, n4, out_0, out_1, out_2,
):
    nc = tc.nc
    with ExitStack() as ctx:
        sb = ctx.enter_context(tc.tile_pool(name="sb", bufs=1))
        ps = ctx.enter_context(tc.psum_pool(name="ps", bufs=1))

        def sbt(shape, dtype, name):
            return sb.tile(shape, dtype, name=name, align_bytes=64)

        def zeroed(width, name):
            tile = sbt([P, width], U8, name)
            nc.gpsimd.memset(tile[:].bitcast(I32), 0)
            return tile

        def load_list(src, name):
            tile = sbt([P, S // GROUP], U16, name)
            nc.sync.dma_start(tile[:], src)
            return tile

        def entries(lists, a, b):
            return lists[:, a // GROUP : b // GROUP]

        def load_column(queue, src, name):
            tile = sbt([P, PACK], F32, name)
            queue.dma_start(out=tile[:], in_=src.rearrange("(p t) o -> p (t o)", t=PACK))
            return tile

        def load_scale_rows(tile, src):
            for r in range(PACK):
                nc.sync.dma_start(out=tile[:].bitcast(I32)[r:P:QUAD, :], in_=src[0].bitcast(I32)[r:SCALE_ROWS:PACK, :])

        def dealt_words(src, name):
            raw = sbt([P, 2 * H], U8, name + "_raw")
            nc.sync.dma_start(out=raw[:].bitcast(I32), in_=src[0].bitcast(I32))
            tile = sbt([P, 2 * H], U8, name)
            nc.scalar.copy(
                out=tile[:].bitcast(U16).rearrange("p (t m) -> p t m", t=PACK),
                in_=raw[:].bitcast(U16).rearrange("p (m t) -> p t m", t=PACK),
            )
            return tile

        def dealt_scales(engine, raw, name, parts):
            tile = sbt([P, H], U8, name)
            for part in parts:
                engine.tensor_copy(
                    out=tile[:].rearrange("p (t m) -> p t m", t=PACK)[:, part, :],
                    in_=raw[:].rearrange("p (m t) -> p t m", t=PACK)[:, part, :],
                )
            return tile

        def interleave(copy, dst, src):
            copy(out=dst.rearrange("p (c i) t -> p c t i", i=4), in_=src.rearrange("p t (c i) -> p c t i", i=4))

        def mx(out, words, scales, t, moving, moving_scales, start, stop):
            nc.tensor.matmul_mx(
                out=out,
                lhsT=words[:, 2 * P * t : 2 * P * (t + 1)].bitcast(FP4X4),
                lhsT_scale=scales[:, P * t : P * (t + 1)],
                rhs=moving.bitcast(FP8X4),
                rhs_scale=moving_scales,
                start=start,
                stop=stop,
            )

        xs = zeroed(T, "xs")
        w1s_raw = zeroed(H, "w1s_raw")
        hz_scales = zeroed(S, "hz_scales")
        w3s_raw = zeroed(H, "w3s_raw")
        w2s_raw = zeroed(H, "w2s_raw")

        offs_t = load_list(offs, "offs_t")
        hz_t = load_list(hz, "hz_t")
        xs_rows = x_scales[0].bitcast(I32)
        for r in range(2):
            nc.sync.dma_start(out=xs[:].bitcast(I32)[r:P:GROUP, :], in_=xs_rows[r:SCALE_ROWS:2, :])
            nc.sync.dma_start(out=xs[:].bitcast(I32)[2 + r : P : QUAD, :], in_=xs_rows[2 + r : SCALE_ROWS : PACK, :])
        xw = sbt([P, T], U32, "xw")
        nc.sync.dma_start(out=xw[:].bitcast(I32), in_=x_words[0].rearrange("p n t -> p (n t)").bitcast(I32))
        w1w = dealt_words(w1_words, "w1w")
        load_scale_rows(w1s_raw, w1_scales)
        tau_t = load_column(nc.scalar, tau, "tau_t")
        w3w = dealt_words(w3_words, "w3w")
        w2w = dealt_words(w2_words, "w2w")
        n2_t = load_list(n2, "n2_t")
        n1_t = load_list(n1, "n1_t")
        gn_t = load_column(nc.sync, gn, "gn_t")
        load_scale_rows(w3s_raw, w3_scales)
        load_scale_rows(w2s_raw, w2_scales)

        xq_scales = sbt([P, S], U8, "xq_scales")
        nc.vector.tensor_copy(xq_scales[:], xs[:].indirect(offs_t[:]))
        hz_bytes = sbt([P, S], U8, "hz_bytes")
        nc.vector.tensor_copy(hz_bytes[:], xs[:].indirect(hz_t[:]))
        xq_words = sbt([P, S], U32, "xq_words")
        nc.vector.tensor_copy(xq_words[:], xw[:].indirect(offs_t[:]))
        w1s = dealt_scales(nc.vector, w1s_raw, "w1s", (slice(0, 1), slice(1, PACK)))
        hz_words = sbt([P, S], U32, "w1s_raw")
        nc.vector.tensor_copy(hz_words[:], xw[:].indirect(hz_t[:]))
        neg_tau = sbt([P, PACK], F32, "neg_tau")
        nc.vector.tensor_scalar(out=neg_tau[:], in0=tau_t[:], scalar1=-1.0, scalar2=None, op0=ALU.mult)

        y, ea_bias = [], []
        for t in range(PACK):
            bank = ps.tile([P, S], F32, name=f"odd_bank{t}")
            mx(bank[:], w1w, w1s, t, xq_words[:], xq_scales[:], True, True)
            y_t = sbt([P, S], F32, f"window{t}")
            low = sbt([P, 1], F32, f"low{t}")
            nc.vector.tensor_scalar(
                out=y_t[:], in0=bank[:], scalar1=1.0, scalar2=None, op0=ALU.mult, op1=ALU.min, accum_out=low[:]
            )
            bias = sbt([P, 1], F32, f"ea_bias{t}")
            nc.vector.tensor_scalar(out=bias[:], in0=low[:], scalar1=tau_t[:, t : t + 1], scalar2=None, op0=ALU.mult)
            y.append(y_t)
            ea_bias.append(bias)
        gn_m2 = sbt([P, PACK], F32, "gn_m2")
        nc.vector.tensor_scalar(out=gn_m2[:], in0=gn_t[:], scalar1=-2.0, scalar2=None, op0=ALU.mult)

        for r, place in enumerate((0, 1, GROUP, GROUP + 1)):
            nc.sync.dma_start(out=hz_scales[:].bitcast(I32)[r:P:QUAD, :], in_=hz_bytes[:].bitcast(I32)[place:P:QUAD, :])
        n3_t = load_list(n3, "n3_t")
        n4_t = load_list(n4, "n4_t")
        w3s = dealt_scales(nc.gpsimd, w3s_raw, "w3s", (slice(0, PACK),))
        w2s = dealt_scales(nc.gpsimd, w2s_raw, "w2s", (slice(0, PACK),))

        h_banks = []
        for c, (a, b) in enumerate(Z_CHUNKS):
            width = b - a
            z = sbt([P, PACK, width], BF16, f"z{c}")
            pulls = []
            for t in range(PACK + 1):
                if t < PACK:
                    y_n2 = sbt([P, width], F32, f"y_n2_{t}")
                    nc.scalar.activation(out=y_n2[:], in_=y[t][:].indirect(entries(n2_t, a, b)), func=ACT.Copy)
                    ea = sbt([P, width], F32, f"ea{t}")
                    nc.scalar.activation(
                        out=ea[:], in_=y[t][:].indirect(entries(n1_t, a, b)), func=ACT.Exp,
                        bias=ea_bias[t][:], scale=neg_tau[:, t : t + 1],
                    )
                    pull = sbt([P, width], F32, f"pull{c}_{t}")
                    nc.vector.scalar_tensor_tensor(
                        out=pull[:], in0=ea[:], scalar=gn_m2[:, t : t + 1], in1=y_n2[:], op0=ALU.mult, op1=ALU.mult
                    )
                    pulls.append(pull)
                if t > 0:
                    u = t - 1
                    nc.vector.scalar_tensor_tensor(
                        out=z[:, u, :], in0=y[u][:, a:b], scalar=gn_t[:, u : u + 1], in1=pulls[u][:],
                        op0=ALU.mult, op1=ALU.add,
                    )
            z_side = sbt([P, width, PACK], BF16, f"z_side{c}")
            interleave(nc.scalar.copy if c == 1 else nc.vector.tensor_copy, z_side[:], z[:])
            z_words = sbt([P, width], U32, f"z_words{c}")
            z_scales = sbt([P, width], U8, f"z_scales{c}")
            nc.vector.quantize_mx(
                out=z_words[:].bitcast(FP8X4), scales=z_scales[:], in_=z_side[:].rearrange("p n t -> p (n t)")
            )
            if c == len(Z_CHUNKS) - 1:
                h = [sbt([P, S], F32, f"window{t}") for t in range(PACK)]
                for t in range(PACK):
                    for (a0, b0), banks in zip(Z_CHUNKS, h_banks):
                        nc.scalar.copy(out=h[t][:, a0:b0], in_=banks[t][:])
            banks = [ps.tile([P, width], F32, name=f"odd_bank{t}" if c % 2 else f"even_bank{t}") for t in range(PACK)]
            for t in range(PACK):
                mx(banks[t][:], w3w, w3s, t, hz_words[:, a:b], hz_scales[:, a:b], True, False)
            for t in range(PACK):
                mx(banks[t][:], w2w, w2s, t, z_words[:], z_scales[:], False, True)
            h_banks.append(banks)
        for t in range(PACK):
            nc.vector.tensor_copy(out=h[t][:, Z_CHUNKS[-1][0] : S], in_=h_banks[-1][t][:])

        looked_up, diffs, weights = [], [], []
        for t in range(PACK):
            pair = sbt([P, 2, S], F32, f"pair{t}")
            for a, b in HALVES:
                nc.scalar.activation(out=pair[:, 1, a:b], in_=h[t][:].indirect(entries(n4_t, a, b)), func=ACT.Copy)
            for a, b in HALVES:
                nc.vector.tensor_copy(pair[:, 0, a:b], h[t][:].indirect(entries(n3_t, a, b)))
            diff = sbt([P, 2, S], F32, f"diff{t}")
            nc.vector.tensor_tensor(
                out=diff[:], in0=pair[:], in1=h[t][:].unsqueeze(1).to_broadcast([P, 2, S]), op=ALU.subtract
            )
            looked_up.append(pair)
            diffs.append(diff)
        den = sbt([P, PACK, S], F32, "den")
        for t in range(PACK):
            square = sbt([P, 2, S], F32, f"square{t}")
            nc.scalar.activation(out=square[:], in_=diffs[t][:], func=ACT.Square)
            kr = sbt([P, 2, S], F32, f"kr{t}")
            nc.scalar.activation(out=kr[:], in_=square[:], func=ACT.Exp, scale=-0.5)
            nc.vector.scalar_tensor_tensor(
                out=den[:, t, :], in0=kr[:, 0, :], scalar=0.5, in1=kr[:, 1, :], op0=ALU.add, op1=ALU.add
            )
            weights.append(kr)
        den_sq = sbt([P, PACK, S], F32, "den_sq")
        for t in range(2):
            nc.scalar.activation(out=den_sq[:, t, :], in_=den[:, t, :], func=ACT.Square)
        num = sbt([P, PACK, S], F32, "num")
        for t0 in range(0, PACK, 2):
            terms = sbt([P, 2, 2, S], F32, f"terms{t0}")
            for u in range(2):
                nc.vector.tensor_tensor(
                    out=terms[:, u, :, :], in0=weights[t0 + u][:], in1=looked_up[t0 + u][:], op=ALU.mult
                )
            for u in range(2):
                nc.vector.tensor_tensor(
                    out=num[:, t0 + u, :], in0=terms[:, u, 0, :], in1=terms[:, u, 1, :], op=ALU.add
                )

        out_rows = out_0.rearrange("(p t) j -> p t j", t=PACK)
        result = sbt([P, PACK, S], F32, "result")
        inverse = sbt([P, 2, S], F32, f"square{PACK - 1}")
        for t in range(2):
            nc.scalar.activation(out=inverse[:, t, :], in_=den_sq[:, t, :], func=ACT.Abs_reciprocal_sqrt)
        nc.vector.tensor_tensor(out=result[:, :2, :], in0=num[:, :2, :], in1=inverse[:], op=ALU.mult)
        nc.sync.dma_start(out=out_rows[:, :2, :], in_=result[:, :2, :])
        for a, b in HALVES:
            nc.scalar.activation(out=den_sq[:, 2:, a:b], in_=den[:, 2:, a:b], func=ACT.Square)
        inverses = []
        for a, b in HALVES:
            inverse = sbt([P, 2, HALF], F32, f"inverse{a}")
            nc.scalar.activation(out=inverse[:], in_=den_sq[:, 2:, a:b], func=ACT.Abs_reciprocal_sqrt)
            inverses.append(inverse)

        out_words = sbt([P, S], U32, "out_words")
        out_scales = sbt([P, S], U8, "out_scales")
        for (a, b), inverse in zip(HALVES, inverses):
            nc.vector.tensor_tensor(out=result[:, 2:, a:b], in0=num[:, 2:, a:b], in1=inverse[:], op=ALU.mult)
            nc.sync.dma_start(out=out_rows[:, 2:, a:b], in_=result[:, 2:, a:b])
            for a0, copy in ((a, nc.scalar.copy), (a + OUT_WIDTH, nc.vector.tensor_copy)):
                columns = slice(a0, a0 + OUT_WIDTH)
                side = sbt([P, OUT_WIDTH, PACK], BF16, f"out_side{a0}")
                interleave(copy, side[:], result[:, :, columns])
                nc.vector.quantize_mx(
                    out=out_words[:, columns].bitcast(FP8X4), scales=out_scales[:, columns],
                    in_=side[:].rearrange("p n t -> p (n t)"),
                )
            nc.sync.dma_start(
                out=out_1[0].rearrange("p n t -> p (n t)").bitcast(I32)[:, a:b], in_=out_words[:, a:b].bitcast(I32)
            )
        for q in range(P // QUAD):
            (nc.scalar if q % 2 else nc.sync).dma_start(
                out=out_2[0].bitcast(I32)[PACK * q : PACK * (q + 1), :],
                in_=out_scales[:].bitcast(I32)[QUAD * q : QUAD * q + PACK, :],
            )
